import numpy as np
import ml_dtypes


def mxq(x, axis, fmt="e4m3"):
    dtype, down = {"e4m3": (ml_dtypes.float8_e4m3fn, 7), "e5m2": (ml_dtypes.float8_e5m2, 14)}[fmt]
    v = np.moveaxis(np.asarray(x, np.float32).astype(ml_dtypes.bfloat16).astype(np.float64), axis, -1)
    blocks = v.reshape(v.shape[:-1] + (-1, 32))
    amax = np.abs(blocks).max(-1, keepdims=True)
    byte = np.maximum(np.where(amax > 0, np.frexp(amax)[1] - 1 + 127, 0) - down, 1)
    scale = np.exp2(byte - 127.0)
    codes = (blocks / scale).astype(np.float32).astype(dtype).astype(np.float64)
    return np.moveaxis((codes * scale).reshape(v.shape), -1, axis)


WIDE = False


def mx_kscale(k):
    if not WIDE:
        return np.ones(k)
    levels = np.array([10, -10, 5, -5, 0])
    if k % 512:
        return np.exp2(np.random.permutation(np.resize(levels, k // 32))).repeat(32)
    a = np.empty((k // 512, 16))
    for p in range(k // 512):
        a[p, :8] = np.random.permutation(np.resize(levels, 8))
        for g in range(8):
            far = levels[np.abs(levels - a[p, g]) >= 10]
            a[p, g + 8] = far[np.random.randint(len(far))]
    return np.exp2(a.ravel()).repeat(32)


def f64(x):
    return np.asarray(x).astype(np.float64)


def striped(idx):
    return np.tile(idx.reshape(-1, 16).T, (8, 1)).astype(np.uint16)


def unstriped(offs):
    return offs[:16].T.reshape(-1).astype(np.int64)


def pack_weight(w):
    k, n = w.shape
    w = f64(np.asarray(w, np.float32).astype(ml_dtypes.bfloat16)).reshape(k // 32, 32, n)
    amax = np.abs(w).max(1)
    byte = np.clip(np.where(amax > 0, np.frexp(amax)[1] - 1 + 127 - 7, 1), 1, 254)
    scaled = (w * np.exp2(127.0 - byte)[:, None, :]).reshape(k, n).astype(np.float32)
    words = np.ascontiguousarray(scaled.reshape(k // 512, 128, 4, n).transpose(0, 1, 3, 2)).astype(ml_dtypes.float8_e4m3fn).view(np.uint8)
    return words, np.ascontiguousarray(byte.astype(np.uint8).reshape(k // 512, 16, n))


def unpack_weight(words, scales):
    g, p, n, _ = words.shape
    vals = np.ascontiguousarray(words).view(ml_dtypes.float8_e4m3fn).astype(np.float64) * np.repeat(np.exp2(scales.astype(np.float64) - 127.0), 8, axis=1)[..., None]
    return vals.transpose(0, 1, 3, 2).reshape(g * 512, n)


def gelu(v):
    return 0.5 * v * (1.0 + np.tanh(np.sqrt(2.0 / np.pi) * (v + 0.044715 * v**3)))


K, T, S, N = 512, 2048, 512, 256


def setup_inputs():
    n = np.random.standard_normal
    s = mx_kscale(K)[:, None]
    w1, w2 = n((2, K, N)) / np.sqrt(2 * K) / s[None]
    packed = pack_weight(n((K, T)) * s)
    return {
        "xT": (n((K, S)) * s).astype(np.float32),
        "s_words": packed[0],
        "s_scales": packed[1],
        "w1": w1.astype(np.float32),
        "w2": w2.astype(np.float32),
        "b": (0.3 * n((N, 1))).astype(np.float32),
        "offs": striped(np.random.permutation(T)[:S]),
    }


def reference(xT, s_words, s_scales, w1, w2, b, offs):
    y = mxq(f64(w1), 0, "e4m3").T @ mxq(f64(xT), 0, "e4m3") + mxq(f64(w2), 0, "e4m3").T @ unpack_weight(s_words, s_scales)[:, unstriped(offs)]
    return gelu(y + f64(b))

@@ -1,0 +1,141 @@
+from contextlib import ExitStack
+
+import concourse.mybir as mybir
+
+K, T, S, N = 512, 2048, 512, 256
+FLOPS = 2 * 2 * K * N * S
+
+F32 = mybir.dt.float32
+BF16 = mybir.dt.bfloat16
+I32 = mybir.dt.int32
+U32 = mybir.dt.uint32
+U16 = mybir.dt.uint16
+U8 = mybir.dt.uint8
+FP8X4 = mybir.dt.float8_e4m3fn_x4
+GELU = mybir.ActivationFunctionType.Gelu_apprx_tanh
+
+P = 128
+PACK = 4
+M_TILES = N // P
+CHUNKS = ((0, 128), (128, 128), (256, 128), (384, 128))
+
+
+def tile_picked_recall_gelu_p_kernel(tc, xT, s_words, s_scales, w1, w2, b, offs, out):
+    nc = tc.nc
+    with ExitStack() as ctx:
+        keep = ctx.enter_context(tc.tile_pool(name="keep", bufs=1))
+        psum = ctx.enter_context(tc.psum_pool(name="psum", bufs=1))
+
+        offsets = keep.tile([P, S // 16], U16, name="offsets")
+        store_words = keep.tile([P, T], I32, name="store_words", align_bytes=64)
+        store_scales = keep.tile([P, T // 4], I32, name="store_scales", align_bytes=64)
+        bias = keep.tile([P, M_TILES], F32, name="bias")
+        warm_in = keep.tile([P, 1], F32, name="warm_in")
+        warm_out = keep.tile([P, 1], F32, name="warm_out")
+        w_raw = [keep.tile([P, PACK, N], F32, name=f"w_raw{i}") for i in range(2)]
+        w_bf = [keep.tile([P, N, PACK], BF16, name=f"w_bf{i}", align_bytes=64) for i in range(2)]
+        w_codes = [keep.tile([P, N], U32, name=f"w_codes{i}", align_bytes=64) for i in range(2)]
+        w_scales = [keep.tile([P, N], U8, name=f"w_scales{i}", align_bytes=64) for i in range(2)]
+        x_raw = [keep.tile([P, PACK, c[1]], F32, name=f"x_raw{i}") for i, c in enumerate(CHUNKS)]
+        x_bf = [keep.tile([P, c[1], PACK], BF16, name=f"x_bf{i}", align_bytes=64) for i, c in enumerate(CHUNKS)]
+        x_codes = [keep.tile([P, c[1]], U32, name=f"x_codes{i}", align_bytes=64) for i, c in enumerate(CHUNKS)]
+        x_scales = [keep.tile([P, c[1]], U8, name=f"x_scales{i}", align_bytes=64) for i, c in enumerate(CHUNKS)]
+        picked_words = keep.tile([P, S], U32, name="picked_words", align_bytes=64)
+        picked_scales = keep.tile([P, S], U8, name="picked_scales", align_bytes=64)
+        result = [keep.tile([P, M_TILES, c[1]], F32, name=f"result{i}") for i, c in enumerate(CHUNKS)]
+        acc = [[psum.tile([P, c[1]], F32, name=f"acc{i}_{m}") for m in range(M_TILES)] for i, c in enumerate(CHUNKS)]
+
+        scale_rows = s_scales[0].bitcast(I32).rearrange("(q r) c -> r q c", r=4)
+        x_rows = xT.rearrange("(p j) s -> p j s", j=PACK)
+        out_rows = out.rearrange("(m p) s -> p m s", p=P)
+
+        def load_words():
+            nc.sync.dma_start(out=store_words[:], in_=s_words[0].rearrange("p c r -> p (c r)").bitcast(I32))
+
+        def load_offs():
+            nc.sync.dma_start(offsets[:], offs)
+
+        def load_scales(r, eng):
+            eng.dma_start(out=store_scales[r:P:32, :], in_=scale_rows[r])
+
+        def load_w(i):
+            nc.sync.dma_start(out=w_raw[i][:], in_=(w1, w2)[i].rearrange("(p j) n -> p j n", j=PACK))
+
+        def load_x(i):
+            c0, cw = CHUNKS[i]
+            nc.sync.dma_start(out=x_raw[i][:], in_=x_rows[:, :, c0:c0 + cw])
+
+        def load_bias(eng):
+            with nc.allow_non_contiguous_dma(reason="one bias value a partition"):
+                eng.dma_start(out=bias[:], in_=b.rearrange("(m p) o -> p (m o)", p=P))
+
+        def interleave(eng, dst, src, lo, hi):
+            o = dst[:, lo:hi, :]
+            s = src[:, :, lo:hi].rearrange("p j w -> p w j")
+            if eng is nc.scalar:
+                nc.scalar.copy(out=o, in_=s)
+            else:
+                nc.vector.tensor_copy(out=o, in_=s)
+
+        def quantize(codes, scales, src):
+            nc.vector.quantize_mx(out=codes[:].bitcast(FP8X4), scales=scales[:], in_=src[:].rearrange("p w j -> p (w j)"))
+
+        def gather_scales():
+            nc.vector.tensor_copy(picked_scales[:], store_scales[:].bitcast(U8).indirect(offsets[:]))
+
+        def gather_words(h):
+            nc.vector.tensor_copy(picked_words[:, 256 * h:256 * (h + 1)], store_words[:].bitcast(U32).indirect(offsets[:, 16 * h:16 * (h + 1)]))
+
+        def mm_store(i, m, start, stop):
+            c0, cw = CHUNKS[i]
+            ms = slice(m * P, (m + 1) * P)
+            nc.tensor.matmul_mx(out=acc[i][m][:], lhsT=w_codes[1][:, ms].bitcast(FP8X4), lhsT_scale=w_scales[1][:, ms],
+                                rhs=picked_words[:, c0:c0 + cw].bitcast(FP8X4), rhs_scale=picked_scales[:, c0:c0 + cw],
+                                start=start, stop=stop)
+
+        def mm_x(i, m, start, stop):
+            ms = slice(m * P, (m + 1) * P)
+            nc.tensor.matmul_mx(out=acc[i][m][:], lhsT=w_codes[0][:, ms].bitcast(FP8X4), lhsT_scale=w_scales[0][:, ms],
+                                rhs=x_codes[i][:].bitcast(FP8X4), rhs_scale=x_scales[i][:],
+                                start=start, stop=stop)
+
+        def gelu(i, m):
+            nc.scalar.activation(out=result[i][:, m, :], in_=acc[i][m][:], func=GELU, bias=bias[:, m:m + 1])
+
+        def store(i):
+            c0, cw = CHUNKS[i]
+            nc.sync.dma_start(out=out_rows[:, :, c0:c0 + cw], in_=result[i][:])
+
+        nc.vector.memset(store_scales[:], 0)
+        nc.vector.memset(warm_in[:], 0.0)
+        load_w(1)
+        load_bias(nc.scalar)
+        load_offs()
+        for r in range(4):
+            load_scales(r, nc.sync)
+        load_words()
+        load_w(0)
+        for i in range(len(CHUNKS)):
+            load_x(i)
+        nc.scalar.activation(out=warm_out[:], in_=warm_in[:], func=GELU)
+        interleave(nc.scalar, w_bf[1], w_raw[1], 0, N)
+        gather_scales()
+        quantize(w_codes[1], w_scales[1], w_bf[1])
+        for h in range(2):
+            gather_words(h)
+            for i in (2 * h, 2 * h + 1):
+                for m in range(M_TILES):
+                    mm_store(i, m, True, False)
+        interleave(nc.scalar, w_bf[0], w_raw[0], 0, 96)
+        interleave(nc.vector, w_bf[0], w_raw[0], 96, N)
+        interleave(nc.scalar, x_bf[0], x_raw[0], 0, 128)
+        quantize(w_codes[0], w_scales[0], w_bf[0])
+        for i in range(len(CHUNKS)):
+            if i + 1 < len(CHUNKS):
+                interleave(nc.vector, x_bf[i + 1], x_raw[i + 1], 0, 128)
+            quantize(x_codes[i], x_scales[i], x_bf[i])
+            for m in range(M_TILES):
+                mm_x(i, m, False, True)
+            for m in range(M_TILES):
+                gelu(i, m)
+            store(i)

@@ -29,8 +29,8 @@ def tile_picked_recall_gelu_p_kernel(tc, xT, s_words, s_scales, w1, w2, b, offs,
         offsets = keep.tile([P, S // 16], U16, name="offsets")
         store_words = keep.tile([P, T], I32, name="store_words", align_bytes=64)
         store_scales = keep.tile([P, T // 4], I32, name="store_scales", align_bytes=64)
-        bias = keep.tile([P, M_TILES], F32, name="bias")
-        warm_in = keep.tile([P, 1], F32, name="warm_in")
+        bias_rows = keep.tile([P, P], F32, name="bias_rows", align_bytes=64)
+        bias = keep.tile([P, P], F32, name="bias", align_bytes=64)
         warm_out = keep.tile([P, 1], F32, name="warm_out")
         w_raw = [keep.tile([P, PACK, N], F32, name=f"w_raw{i}") for i in range(2)]
         w_bf = [keep.tile([P, N, PACK], BF16, name=f"w_bf{i}", align_bytes=64) for i in range(2)]
@@ -66,8 +66,8 @@ def tile_picked_recall_gelu_p_kernel(tc, xT, s_words, s_scales, w1, w2, b, offs,
             nc.sync.dma_start(out=x_raw[i][:], in_=x_rows[:, :, c0:c0 + cw])
 
         def load_bias(eng):
-            with nc.allow_non_contiguous_dma(reason="one bias value a partition"):
-                eng.dma_start(out=bias[:], in_=b.rearrange("(m p) o -> p (m o)", p=P))
+            eng.dma_start(out=bias_rows[0:P:32, 0:32 * M_TILES].rearrange("q (m i) -> q m i", i=32),
+                          in_=b.rearrange("(m q i) o -> q m (i o)", q=4, i=32))
 
         def interleave(eng, dst, src, lo, hi):
             o = dst[:, lo:hi, :]
@@ -100,14 +100,18 @@ def tile_picked_recall_gelu_p_kernel(tc, xT, s_words, s_scales, w1, w2, b, offs,
                                 start=start, stop=stop)
 
         def gelu(i, m):
-            nc.scalar.activation(out=result[i][:, m, :], in_=acc[i][m][:], func=GELU, bias=bias[:, m:m + 1])
+            nc.scalar.activation(out=result[i][:, m, :], in_=acc[i][m][:], func=GELU, bias=bias[:, 32 * m:32 * m + 1])
+
+        def store_m(i, m, eng):
+            c0, cw = CHUNKS[i]
+            eng.dma_start(out=out_rows[:, m, c0:c0 + cw], in_=result[i][:, m, :])
 
         def store(i):
             c0, cw = CHUNKS[i]
             nc.sync.dma_start(out=out_rows[:, :, c0:c0 + cw], in_=result[i][:])
 
+        nc.vector.memset(bias_rows[:], 0.0)
         nc.vector.memset(store_scales[:], 0)
-        nc.vector.memset(warm_in[:], 0.0)
         load_w(1)
         load_bias(nc.scalar)
         load_offs()
@@ -117,7 +121,8 @@ def tile_picked_recall_gelu_p_kernel(tc, xT, s_words, s_scales, w1, w2, b, offs,
         load_w(0)
         for i in range(len(CHUNKS)):
             load_x(i)
-        nc.scalar.activation(out=warm_out[:], in_=warm_in[:], func=GELU)
+        nc.scalar.activation(out=warm_out[:], in_=bias_rows[:, P - 1:P], func=GELU)
+        nc.vector.transpose(bias[:], bias_rows[:])
         interleave(nc.scalar, w_bf[1], w_raw[1], 0, N)
         gather_scales()
         quantize(w_codes[1], w_scales[1], w_bf[1])
@@ -129,13 +134,18 @@ def tile_picked_recall_gelu_p_kernel(tc, xT, s_words, s_scales, w1, w2, b, offs,
         interleave(nc.scalar, w_bf[0], w_raw[0], 0, 96)
         interleave(nc.vector, w_bf[0], w_raw[0], 96, N)
         interleave(nc.scalar, x_bf[0], x_raw[0], 0, 128)
+        interleave(nc.scalar, x_bf[1], x_raw[1], 0, 128)
         quantize(w_codes[0], w_scales[0], w_bf[0])
         for i in range(len(CHUNKS)):
-            if i + 1 < len(CHUNKS):
+            if 2 <= i + 1 < len(CHUNKS):
                 interleave(nc.vector, x_bf[i + 1], x_raw[i + 1], 0, 128)
             quantize(x_codes[i], x_scales[i], x_bf[i])
             for m in range(M_TILES):
                 mm_x(i, m, False, True)
             for m in range(M_TILES):
                 gelu(i, m)
-            store(i)
+            if i + 1 < len(CHUNKS):
+                store(i)
+            else:
+                store_m(i, 0, nc.sync)
+                store_m(i, 1, nc.scalar)

@@ -70,8 +70,8 @@ def tile_picked_recall_gelu_p_kernel(tc, xT, s_words, s_scales, w1, w2, b, offs,
                           in_=b.rearrange("(m q i) o -> q m (i o)", q=4, i=32))
 
         def interleave(eng, dst, src, lo, hi):
-            o = dst[:, lo:hi, :]
-            s = src[:, :, lo:hi].rearrange("p j w -> p w j")
+            o = dst[:, lo:hi, :].rearrange("p (c i) j -> p c j i", i=4)
+            s = src[:, :, lo:hi].rearrange("p j (c i) -> p c j i", i=4)
             if eng is nc.scalar:
                 nc.scalar.copy(out=o, in_=s)
             else:

@@ -18,6 +18,7 @@ P = 128
 PACK = 4
 M_TILES = N // P
 CHUNKS = ((0, 128), (128, 128), (256, 128), (384, 128))
+LOADS = ((0, 256), (256, 128), (384, 128))
 
 
 def tile_picked_recall_gelu_p_kernel(tc, xT, s_words, s_scales, w1, w2, b, offs, out):
@@ -28,15 +29,16 @@ def tile_picked_recall_gelu_p_kernel(tc, xT, s_words, s_scales, w1, w2, b, offs,
 
         offsets = keep.tile([P, S // 16], U16, name="offsets")
         store_words = keep.tile([P, T], I32, name="store_words", align_bytes=64)
-        store_scales = keep.tile([P, T // 4], I32, name="store_scales", align_bytes=64)
+        store_scales = keep.tile([P, T // 4], I32, name="store_scales", tag="scale_bytes", align_bytes=64)
         bias_rows = keep.tile([P, P], F32, name="bias_rows", align_bytes=64)
         bias = keep.tile([P, P], F32, name="bias", align_bytes=64)
         warm_out = keep.tile([P, 1], F32, name="warm_out")
         w_raw = [keep.tile([P, PACK, N], F32, name=f"w_raw{i}") for i in range(2)]
         w_bf = [keep.tile([P, N, PACK], BF16, name=f"w_bf{i}", align_bytes=64) for i in range(2)]
-        w_codes = [keep.tile([P, N], U32, name=f"w_codes{i}", align_bytes=64) for i in range(2)]
+        w_codes = [keep.tile([P, N], U32, name="w_codes0", align_bytes=64)]
         w_scales = [keep.tile([P, N], U8, name=f"w_scales{i}", align_bytes=64) for i in range(2)]
-        x_raw = [keep.tile([P, PACK, c[1]], F32, name=f"x_raw{i}") for i, c in enumerate(CHUNKS)]
+        x_loads = [keep.tile([P, PACK, c[1]], F32, name=f"x_load{i}") for i, c in enumerate(LOADS)]
+        x_raw = [[x_loads[k][:, :, c[0] - a[0]:c[0] - a[0] + c[1]] for k, a in enumerate(LOADS) if a[0] <= c[0] < a[0] + a[1]][0] for c in CHUNKS]
         x_bf = [keep.tile([P, c[1], PACK], BF16, name=f"x_bf{i}", align_bytes=64) for i, c in enumerate(CHUNKS)]
         x_codes = [keep.tile([P, c[1]], U32, name=f"x_codes{i}", align_bytes=64) for i, c in enumerate(CHUNKS)]
         x_scales = [keep.tile([P, c[1]], U8, name=f"x_scales{i}", align_bytes=64) for i, c in enumerate(CHUNKS)]
@@ -62,8 +64,8 @@ def tile_picked_recall_gelu_p_kernel(tc, xT, s_words, s_scales, w1, w2, b, offs,
             nc.sync.dma_start(out=w_raw[i][:], in_=(w1, w2)[i].rearrange("(p j) n -> p j n", j=PACK))
 
         def load_x(i):
-            c0, cw = CHUNKS[i]
-            nc.sync.dma_start(out=x_raw[i][:], in_=x_rows[:, :, c0:c0 + cw])
+            c0, cw = LOADS[i]
+            nc.sync.dma_start(out=x_loads[i][:], in_=x_rows[:, :, c0:c0 + cw])
 
         def load_bias(eng):
             eng.dma_start(out=bias_rows[0:P:32, 0:32 * M_TILES].rearrange("q (m i) -> q m i", i=32),
@@ -119,26 +121,35 @@ def tile_picked_recall_gelu_p_kernel(tc, xT, s_words, s_scales, w1, w2, b, offs,
             load_scales(r, nc.sync)
         load_words()
         load_w(0)
-        for i in range(len(CHUNKS)):
+        for i in range(len(LOADS)):
             load_x(i)
         nc.scalar.activation(out=warm_out[:], in_=bias_rows[:, P - 1:P], func=GELU)
         nc.vector.transpose(bias[:], bias_rows[:])
         interleave(nc.scalar, w_bf[1], w_raw[1], 0, N)
         gather_scales()
+        w_codes.append(keep.tile([P, N], U32, name="w_codes1", tag="scale_bytes", align_bytes=64))
         quantize(w_codes[1], w_scales[1], w_bf[1])
         for h in range(2):
             gather_words(h)
             for i in (2 * h, 2 * h + 1):
                 for m in range(M_TILES):
                     mm_store(i, m, True, False)
-        interleave(nc.scalar, w_bf[0], w_raw[0], 0, 96)
-        interleave(nc.vector, w_bf[0], w_raw[0], 96, N)
-        interleave(nc.scalar, x_bf[0], x_raw[0], 0, 128)
-        interleave(nc.scalar, x_bf[1], x_raw[1], 0, 128)
+        interleave(nc.scalar, w_bf[0], w_raw[0], 0, 128)
+        interleave(nc.vector, w_bf[0], w_raw[0], 128, N)
+        scalar_cols = (0,128,0,0)
+
+        def round_x(i):
+            if scalar_cols[i] > 0:
+                interleave(nc.scalar, x_bf[i], x_raw[i], 0, scalar_cols[i])
+            if scalar_cols[i] < 128:
+                interleave(nc.vector, x_bf[i], x_raw[i], scalar_cols[i], 128)
+
+        round_x(0)
+        round_x(1)
         quantize(w_codes[0], w_scales[0], w_bf[0])
         for i in range(len(CHUNKS)):
             if 2 <= i + 1 < len(CHUNKS):
-                interleave(nc.vector, x_bf[i + 1], x_raw[i + 1], 0, 128)
+                round_x(i + 1)
             quantize(x_codes[i], x_scales[i], x_bf[i])
             for m in range(M_TILES):
                 mm_x(i, m, False, True)

@@ -134,9 +134,9 @@ def tile_picked_recall_gelu_p_kernel(tc, xT, s_words, s_scales, w1, w2, b, offs,
             for i in (2 * h, 2 * h + 1):
                 for m in range(M_TILES):
                     mm_store(i, m, True, False)
-        interleave(nc.scalar, w_bf[0], w_raw[0], 0, 128)
-        interleave(nc.vector, w_bf[0], w_raw[0], 128, N)
-        scalar_cols = (0,128,0,0)
+        interleave(nc.scalar, w_bf[0], w_raw[0], 0, 96)
+        interleave(nc.vector, w_bf[0], w_raw[0], 96, N)
+        scalar_cols = (0,128,128,0)
 
         def round_x(i):
             if scalar_cols[i] > 0:

@@ -16,9 +16,17 @@ GELU = mybir.ActivationFunctionType.Gelu_apprx_tanh
 
 P = 128
 PACK = 4
+QUADRANT = 32
 M_TILES = N // P
-CHUNKS = ((0, 128), (128, 128), (256, 128), (384, 128))
-LOADS = ((0, 256), (256, 128), (384, 128))
+CHUNK = 128
+CHUNKS = S // CHUNK
+LAST = CHUNKS - 1
+GATHER = 256
+LIST_ROWS = 16
+X_LOADS = ((0, 2 * CHUNK), (2 * CHUNK, CHUNK), (3 * CHUNK, CHUNK))
+W1_SCALAR_COLS = 128
+X_SCALAR_COLS = (CHUNK // 2, CHUNK // 2, CHUNK, 0)
+LAST_PARTS = ((0, CHUNK // 2), (CHUNK // 2, CHUNK))
 
 
 def tile_picked_recall_gelu_p_kernel(tc, xT, s_words, s_scales, w1, w2, b, offs, out):
@@ -27,136 +35,103 @@ def tile_picked_recall_gelu_p_kernel(tc, xT, s_words, s_scales, w1, w2, b, offs,
         keep = ctx.enter_context(tc.tile_pool(name="keep", bufs=1))
         psum = ctx.enter_context(tc.psum_pool(name="psum", bufs=1))
 
-        offsets = keep.tile([P, S // 16], U16, name="offsets")
+        offsets = keep.tile([P, S // LIST_ROWS], U16, name="offsets")
         store_words = keep.tile([P, T], I32, name="store_words", align_bytes=64)
         store_scales = keep.tile([P, T // 4], I32, name="store_scales", tag="scale_bytes", align_bytes=64)
         bias_rows = keep.tile([P, P], F32, name="bias_rows", align_bytes=64)
         bias = keep.tile([P, P], F32, name="bias", align_bytes=64)
         warm_out = keep.tile([P, 1], F32, name="warm_out")
-        w_raw = [keep.tile([P, PACK, N], F32, name=f"w_raw{i}") for i in range(2)]
-        w_bf = [keep.tile([P, N, PACK], BF16, name=f"w_bf{i}", align_bytes=64) for i in range(2)]
-        w_codes = [keep.tile([P, N], U32, name="w_codes0", align_bytes=64)]
-        w_scales = [keep.tile([P, N], U8, name=f"w_scales{i}", align_bytes=64) for i in range(2)]
-        x_loads = [keep.tile([P, PACK, c[1]], F32, name=f"x_load{i}") for i, c in enumerate(LOADS)]
-        x_raw = [[x_loads[k][:, :, c[0] - a[0]:c[0] - a[0] + c[1]] for k, a in enumerate(LOADS) if a[0] <= c[0] < a[0] + a[1]][0] for c in CHUNKS]
-        x_bf = [keep.tile([P, c[1], PACK], BF16, name=f"x_bf{i}", align_bytes=64) for i, c in enumerate(CHUNKS)]
-        x_codes = [keep.tile([P, c[1]], U32, name=f"x_codes{i}", align_bytes=64) for i, c in enumerate(CHUNKS)]
-        x_scales = [keep.tile([P, c[1]], U8, name=f"x_scales{i}", align_bytes=64) for i, c in enumerate(CHUNKS)]
+        w1_raw = keep.tile([P, PACK, N], F32, name="w_raw0")
+        w2_raw = keep.tile([P, PACK, N], F32, name="w_raw1")
+        w1_bf = keep.tile([P, N, PACK], BF16, name="w_bf0", align_bytes=64)
+        w2_bf = keep.tile([P, N, PACK], BF16, name="w_bf1", align_bytes=64)
+        w1_codes = keep.tile([P, N], U32, name="w_codes0", align_bytes=64)
+        w1_scales = keep.tile([P, N], U8, name="w_scales0", align_bytes=64)
+        w2_scales = keep.tile([P, N], U8, name="w_scales1", align_bytes=64)
+        x_loads = [keep.tile([P, PACK, width], F32, name=f"x_load{n}") for n, (first, width) in enumerate(X_LOADS)]
+        x_bf = [keep.tile([P, CHUNK, PACK], BF16, name=f"x_bf{i}", align_bytes=64) for i in range(CHUNKS)]
+        x_codes = [keep.tile([P, CHUNK], U32, name=f"x_codes{i}", align_bytes=64) for i in range(CHUNKS)]
+        x_scales = [keep.tile([P, CHUNK], U8, name=f"x_scales{i}", align_bytes=64) for i in range(CHUNKS)]
         picked_words = keep.tile([P, S], U32, name="picked_words", align_bytes=64)
         picked_scales = keep.tile([P, S], U8, name="picked_scales", align_bytes=64)
-        result = [keep.tile([P, M_TILES, c[1]], F32, name=f"result{i}") for i, c in enumerate(CHUNKS)]
-        acc = [[psum.tile([P, c[1]], F32, name=f"acc{i}_{m}") for m in range(M_TILES)] for i, c in enumerate(CHUNKS)]
+        result = [keep.tile([P, M_TILES, CHUNK], F32, name=f"result{i}") for i in range(CHUNKS)]
+        acc = [[psum.tile([P, CHUNK], F32, name=f"acc{i}_{m}") for m in range(M_TILES)] for i in range(CHUNKS)]
 
-        scale_rows = s_scales[0].bitcast(I32).rearrange("(q r) c -> r q c", r=4)
+        x_raw = [x_loads[n][:, :, c:c + CHUNK] for n, (first, width) in enumerate(X_LOADS) for c in range(0, width, CHUNK)]
         x_rows = xT.rearrange("(p j) s -> p j s", j=PACK)
         out_rows = out.rearrange("(m p) s -> p m s", p=P)
 
-        def load_words():
-            nc.sync.dma_start(out=store_words[:], in_=s_words[0].rearrange("p c r -> p (c r)").bitcast(I32))
-
-        def load_offs():
-            nc.sync.dma_start(offsets[:], offs)
-
-        def load_scales(r, eng):
-            eng.dma_start(out=store_scales[r:P:32, :], in_=scale_rows[r])
-
-        def load_w(i):
-            nc.sync.dma_start(out=w_raw[i][:], in_=(w1, w2)[i].rearrange("(p j) n -> p j n", j=PACK))
-
-        def load_x(i):
-            c0, cw = LOADS[i]
-            nc.sync.dma_start(out=x_loads[i][:], in_=x_rows[:, :, c0:c0 + cw])
-
-        def load_bias(eng):
-            eng.dma_start(out=bias_rows[0:P:32, 0:32 * M_TILES].rearrange("q (m i) -> q m i", i=32),
-                          in_=b.rearrange("(m q i) o -> q m (i o)", q=4, i=32))
-
         def interleave(eng, dst, src, lo, hi):
-            o = dst[:, lo:hi, :].rearrange("p (c i) j -> p c j i", i=4)
-            s = src[:, :, lo:hi].rearrange("p j (c i) -> p c j i", i=4)
+            dst_view = dst[:, lo:hi, :].rearrange("p (c i) j -> p c j i", i=4)
+            src_view = src[:, :, lo:hi].rearrange("p j (c i) -> p c j i", i=4)
             if eng is nc.scalar:
-                nc.scalar.copy(out=o, in_=s)
+                nc.scalar.copy(out=dst_view, in_=src_view)
             else:
-                nc.vector.tensor_copy(out=o, in_=s)
+                nc.vector.tensor_copy(out=dst_view, in_=src_view)
+
+        def round_x(i):
+            if X_SCALAR_COLS[i] > 0:
+                interleave(nc.scalar, x_bf[i], x_raw[i], 0, X_SCALAR_COLS[i])
+            if X_SCALAR_COLS[i] < CHUNK:
+                for lo, hi in LAST_PARTS if i == LAST else ((X_SCALAR_COLS[i], CHUNK),):
+                    interleave(nc.vector, x_bf[i], x_raw[i], lo, hi)
 
         def quantize(codes, scales, src):
-            nc.vector.quantize_mx(out=codes[:].bitcast(FP8X4), scales=scales[:], in_=src[:].rearrange("p w j -> p (w j)"))
+            nc.vector.quantize_mx(out=codes.bitcast(FP8X4), scales=scales, in_=src.rearrange("p c j -> p (c j)"))
 
-        def gather_scales():
-            nc.vector.tensor_copy(picked_scales[:], store_scales[:].bitcast(U8).indirect(offsets[:]))
-
-        def gather_words(h):
-            nc.vector.tensor_copy(picked_words[:, 256 * h:256 * (h + 1)], store_words[:].bitcast(U32).indirect(offsets[:, 16 * h:16 * (h + 1)]))
-
-        def mm_store(i, m, start, stop):
-            c0, cw = CHUNKS[i]
-            ms = slice(m * P, (m + 1) * P)
-            nc.tensor.matmul_mx(out=acc[i][m][:], lhsT=w_codes[1][:, ms].bitcast(FP8X4), lhsT_scale=w_scales[1][:, ms],
-                                rhs=picked_words[:, c0:c0 + cw].bitcast(FP8X4), rhs_scale=picked_scales[:, c0:c0 + cw],
-                                start=start, stop=stop)
-
-        def mm_x(i, m, start, stop):
-            ms = slice(m * P, (m + 1) * P)
-            nc.tensor.matmul_mx(out=acc[i][m][:], lhsT=w_codes[0][:, ms].bitcast(FP8X4), lhsT_scale=w_scales[0][:, ms],
-                                rhs=x_codes[i][:].bitcast(FP8X4), rhs_scale=x_scales[i][:],
-                                start=start, stop=stop)
-
-        def gelu(i, m):
-            nc.scalar.activation(out=result[i][:, m, :], in_=acc[i][m][:], func=GELU, bias=bias[:, 32 * m:32 * m + 1])
-
-        def store_m(i, m, eng):
-            c0, cw = CHUNKS[i]
-            eng.dma_start(out=out_rows[:, m, c0:c0 + cw], in_=result[i][:, m, :])
-
-        def store(i):
-            c0, cw = CHUNKS[i]
-            nc.sync.dma_start(out=out_rows[:, :, c0:c0 + cw], in_=result[i][:])
+        def product(i, m, w_codes, w_scales, codes, scales, first):
+            rows = slice(m * P, (m + 1) * P)
+            nc.tensor.matmul_mx(out=acc[i][m][:], lhsT=w_codes[:, rows].bitcast(FP8X4), lhsT_scale=w_scales[:, rows],
+                                rhs=codes.bitcast(FP8X4), rhs_scale=scales, start=first, stop=not first)
 
         nc.vector.memset(bias_rows[:], 0.0)
         nc.vector.memset(store_scales[:], 0)
-        load_w(1)
-        load_bias(nc.scalar)
-        load_offs()
+
+        nc.sync.dma_start(out=w2_raw[:], in_=w2.rearrange("(p j) n -> p j n", j=PACK))
+        nc.scalar.dma_start(out=bias_rows[0:P:QUADRANT, 0:QUADRANT * M_TILES].rearrange("q (m i) -> q m i", i=QUADRANT),
+                            in_=b.rearrange("(m q i) o -> q m (i o)", q=P // QUADRANT, i=QUADRANT))
+        nc.sync.dma_start(offsets[:], offs)
+        scale_rows = s_scales[0].bitcast(I32).rearrange("(q r) c -> r q c", r=4)
         for r in range(4):
-            load_scales(r, nc.sync)
-        load_words()
-        load_w(0)
-        for i in range(len(LOADS)):
-            load_x(i)
+            nc.sync.dma_start(out=store_scales[r:P:QUADRANT, :], in_=scale_rows[r])
+        nc.sync.dma_start(out=store_words[:], in_=s_words[0].rearrange("p c r -> p (c r)").bitcast(I32))
+        nc.sync.dma_start(out=w1_raw[:], in_=w1.rearrange("(p j) n -> p j n", j=PACK))
+        for n, (first, width) in enumerate(X_LOADS):
+            nc.sync.dma_start(out=x_loads[n][:], in_=x_rows[:, :, first:first + width])
+
         nc.scalar.activation(out=warm_out[:], in_=bias_rows[:, P - 1:P], func=GELU)
         nc.vector.transpose(bias[:], bias_rows[:])
-        interleave(nc.scalar, w_bf[1], w_raw[1], 0, N)
-        gather_scales()
-        w_codes.append(keep.tile([P, N], U32, name="w_codes1", tag="scale_bytes", align_bytes=64))
-        quantize(w_codes[1], w_scales[1], w_bf[1])
-        for h in range(2):
-            gather_words(h)
-            for i in (2 * h, 2 * h + 1):
+
+        interleave(nc.scalar, w2_bf, w2_raw, 0, N)
+        nc.vector.tensor_copy(picked_scales[:], store_scales[:].bitcast(U8).indirect(offsets[:]))
+        w2_codes = keep.tile([P, N], U32, name="w_codes1", tag="scale_bytes", align_bytes=64)
+        quantize(w2_codes[:], w2_scales[:], w2_bf[:])
+        for g0 in range(0, S, GATHER):
+            entries = offsets[:, g0 // LIST_ROWS:(g0 + GATHER) // LIST_ROWS]
+            nc.vector.tensor_copy(picked_words[:, g0:g0 + GATHER], store_words[:].bitcast(U32).indirect(entries))
+            for i in range(g0 // CHUNK, (g0 + GATHER) // CHUNK):
+                cols = slice(i * CHUNK, (i + 1) * CHUNK)
                 for m in range(M_TILES):
-                    mm_store(i, m, True, False)
-        interleave(nc.scalar, w_bf[0], w_raw[0], 0, 96)
-        interleave(nc.vector, w_bf[0], w_raw[0], 96, N)
-        scalar_cols = (0,128,128,0)
+                    product(i, m, w2_codes, w2_scales, picked_words[:, cols], picked_scales[:, cols], first=True)
 
-        def round_x(i):
-            if scalar_cols[i] > 0:
-                interleave(nc.scalar, x_bf[i], x_raw[i], 0, scalar_cols[i])
-            if scalar_cols[i] < 128:
-                interleave(nc.vector, x_bf[i], x_raw[i], scalar_cols[i], 128)
-
+        interleave(nc.scalar, w1_bf, w1_raw, 0, W1_SCALAR_COLS)
+        interleave(nc.vector, w1_bf, w1_raw, W1_SCALAR_COLS, N)
         round_x(0)
         round_x(1)
-        quantize(w_codes[0], w_scales[0], w_bf[0])
-        for i in range(len(CHUNKS)):
-            if 2 <= i + 1 < len(CHUNKS):
+        quantize(w1_codes[:], w1_scales[:], w1_bf[:])
+        for i in range(CHUNKS):
+            if 1 <= i < LAST:
                 round_x(i + 1)
-            quantize(x_codes[i], x_scales[i], x_bf[i])
+            for lo, hi in LAST_PARTS if i == LAST else ((0, CHUNK),):
+                quantize(x_codes[i][:, lo:hi], x_scales[i][:, lo:hi], x_bf[i][:, lo:hi, :])
             for m in range(M_TILES):
-                mm_x(i, m, False, True)
+                product(i, m, w1_codes, w1_scales, x_codes[i][:], x_scales[i][:], first=False)
             for m in range(M_TILES):
-                gelu(i, m)
-            if i + 1 < len(CHUNKS):
-                store(i)
+                nc.scalar.activation(out=result[i][:, m, :], in_=acc[i][m][:], func=GELU,
+                                     bias=bias[:, QUADRANT * m:QUADRANT * m + 1])
+            cols = slice(i * CHUNK, (i + 1) * CHUNK)
+            if i < LAST:
+                nc.sync.dma_start(out=out_rows[:, :, cols], in_=result[i][:])
             else:
-                store_m(i, 0, nc.sync)
-                store_m(i, 1, nc.scalar)
+                nc.sync.dma_start(out=out_rows[:, 0, cols], in_=result[i][:, 0, :])
+                nc.scalar.dma_start(out=out_rows[:, 1, cols], in_=result[i][:, 1, :])

@@ -25,7 +25,7 @@ GATHER = 256
 LIST_ROWS = 16
 X_LOADS = ((0, 2 * CHUNK), (2 * CHUNK, CHUNK), (3 * CHUNK, CHUNK))
 W1_SCALAR_COLS = 128
-X_SCALAR_COLS = (CHUNK // 2, CHUNK // 2, CHUNK, 0)
+X_SCALAR_COLS = (CHUNK // 4, CHUNK // 4, CHUNK, 0)
 LAST_PARTS = ((0, CHUNK // 2), (CHUNK // 2, CHUNK))
 
 
@@ -130,8 +130,4 @@ def tile_picked_recall_gelu_p_kernel(tc, xT, s_words, s_scales, w1, w2, b, offs,
                 nc.scalar.activation(out=result[i][:, m, :], in_=acc[i][m][:], func=GELU,
                                      bias=bias[:, QUADRANT * m:QUADRANT * m + 1])
             cols = slice(i * CHUNK, (i + 1) * CHUNK)
-            if i < LAST:
-                nc.sync.dma_start(out=out_rows[:, :, cols], in_=result[i][:])
-            else:
-                nc.sync.dma_start(out=out_rows[:, 0, cols], in_=result[i][:, 0, :])
-                nc.scalar.dma_start(out=out_rows[:, 1, cols], in_=result[i][:, 1, :])
+            nc.sync.dma_start(out=out_rows[:, :, cols], in_=result[i][:])

@@ -21,11 +21,11 @@ M_TILES = N // P
 CHUNK = 128
 CHUNKS = S // CHUNK
 LAST = CHUNKS - 1
-GATHER = 256
+GATHER = 512
 LIST_ROWS = 16
 X_LOADS = ((0, 2 * CHUNK), (2 * CHUNK, CHUNK), (3 * CHUNK, CHUNK))
-W1_SCALAR_COLS = 128
-X_SCALAR_COLS = (CHUNK // 4, CHUNK // 4, CHUNK, 0)
+W1_SCALAR_COLS = 176
+X_SCALAR_COLS = (48, 48, CHUNK, 0)
 LAST_PARTS = ((0, CHUNK // 2), (CHUNK // 2, CHUNK))
 
 
@@ -114,11 +114,14 @@ def tile_picked_recall_gelu_p_kernel(tc, xT, s_words, s_scales, w1, w2, b, offs,
                 for m in range(M_TILES):
                     product(i, m, w2_codes, w2_scales, picked_words[:, cols], picked_scales[:, cols], first=True)
 
-        interleave(nc.scalar, w1_bf, w1_raw, 0, W1_SCALAR_COLS)
+        interleave(nc.scalar, w1_bf, w1_raw, 0, P)
+        interleave(nc.scalar, w1_bf, w1_raw, P, W1_SCALAR_COLS)
         interleave(nc.vector, w1_bf, w1_raw, W1_SCALAR_COLS, N)
+        for m in range(M_TILES):
+            rows = slice(m * P, (m + 1) * P)
+            quantize(w1_codes[:, rows], w1_scales[:, rows], w1_bf[:, rows, :])
         round_x(0)
         round_x(1)
-        quantize(w1_codes[:], w1_scales[:], w1_bf[:])
         for i in range(CHUNKS):
             if 1 <= i < LAST:
                 round_x(i + 1)

@@ -17,6 +17,7 @@ GELU = mybir.ActivationFunctionType.Gelu_apprx_tanh
 P = 128
 PACK = 4
 QUADRANT = 32
+DMA_ALIGN = 256
 M_TILES = N // P
 CHUNK = 128
 CHUNKS = S // CHUNK
@@ -35,26 +36,27 @@ def tile_picked_recall_gelu_p_kernel(tc, xT, s_words, s_scales, w1, w2, b, offs,
         keep = ctx.enter_context(tc.tile_pool(name="keep", bufs=1))
         psum = ctx.enter_context(tc.psum_pool(name="psum", bufs=1))
 
-        offsets = keep.tile([P, S // LIST_ROWS], U16, name="offsets")
-        store_words = keep.tile([P, T], I32, name="store_words", align_bytes=64)
-        store_scales = keep.tile([P, T // 4], I32, name="store_scales", tag="scale_bytes", align_bytes=64)
-        bias_rows = keep.tile([P, P], F32, name="bias_rows", align_bytes=64)
+        offsets = keep.tile([P, S // LIST_ROWS], U16, name="offsets", align_bytes=DMA_ALIGN)
+        store_words = keep.tile([P, T], I32, name="store_words", align_bytes=DMA_ALIGN)
+        store_scales = keep.tile([P, T // 4], I32, name="store_scales", tag="scale_bytes", align_bytes=DMA_ALIGN)
+        bias_rows = keep.tile([P, P], F32, name="bias_rows", align_bytes=DMA_ALIGN)
         bias = keep.tile([P, P], F32, name="bias", align_bytes=64)
         warm_out = keep.tile([P, 1], F32, name="warm_out")
-        w1_raw = keep.tile([P, PACK, N], F32, name="w_raw0")
-        w2_raw = keep.tile([P, PACK, N], F32, name="w_raw1")
+        w1_raw = keep.tile([P, PACK, N], F32, name="w_raw0", align_bytes=DMA_ALIGN)
+        w2_raw = keep.tile([P, PACK, N], F32, name="w_raw1", align_bytes=DMA_ALIGN)
         w1_bf = keep.tile([P, N, PACK], BF16, name="w_bf0", align_bytes=64)
         w2_bf = keep.tile([P, N, PACK], BF16, name="w_bf1", align_bytes=64)
         w1_codes = keep.tile([P, N], U32, name="w_codes0", align_bytes=64)
         w1_scales = keep.tile([P, N], U8, name="w_scales0", align_bytes=64)
         w2_scales = keep.tile([P, N], U8, name="w_scales1", align_bytes=64)
-        x_loads = [keep.tile([P, PACK, width], F32, name=f"x_load{n}") for n, (first, width) in enumerate(X_LOADS)]
+        x_loads = [keep.tile([P, PACK, width], F32, name=f"x_load{n}", align_bytes=DMA_ALIGN)
+                   for n, (first, width) in enumerate(X_LOADS)]
         x_bf = [keep.tile([P, CHUNK, PACK], BF16, name=f"x_bf{i}", align_bytes=64) for i in range(CHUNKS)]
         x_codes = [keep.tile([P, CHUNK], U32, name=f"x_codes{i}", align_bytes=64) for i in range(CHUNKS)]
         x_scales = [keep.tile([P, CHUNK], U8, name=f"x_scales{i}", align_bytes=64) for i in range(CHUNKS)]
         picked_words = keep.tile([P, S], U32, name="picked_words", align_bytes=64)
         picked_scales = keep.tile([P, S], U8, name="picked_scales", align_bytes=64)
-        result = [keep.tile([P, M_TILES, CHUNK], F32, name=f"result{i}") for i in range(CHUNKS)]
+        result = [keep.tile([P, M_TILES, CHUNK], F32, name=f"result{i}", align_bytes=DMA_ALIGN) for i in range(CHUNKS)]
         acc = [[psum.tile([P, CHUNK], F32, name=f"acc{i}_{m}") for m in range(M_TILES)] for i in range(CHUNKS)]
 
         x_raw = [x_loads[n][:, :, c:c + CHUNK] for n, (first, width) in enumerate(X_LOADS) for c in range(0, width, CHUNK)]
@@ -104,7 +106,7 @@ def tile_picked_recall_gelu_p_kernel(tc, xT, s_words, s_scales, w1, w2, b, offs,
 
         interleave(nc.scalar, w2_bf, w2_raw, 0, N)
         nc.vector.tensor_copy(picked_scales[:], store_scales[:].bitcast(U8).indirect(offsets[:]))
-        w2_codes = keep.tile([P, N], U32, name="w_codes1", tag="scale_bytes", align_bytes=64)
+        w2_codes = keep.tile([P, N], U32, name="w_codes1", tag="scale_bytes", align_bytes=DMA_ALIGN)
         quantize(w2_codes[:], w2_scales[:], w2_bf[:])
         for g0 in range(0, S, GATHER):
             entries = offsets[:, g0 // LIST_ROWS:(g0 + GATHER) // LIST_ROWS]

@@ -18,6 +18,7 @@ P = 128
 PACK = 4
 QUADRANT = 32
 DMA_ALIGN = 256
+SPREAD = 8
 M_TILES = N // P
 CHUNK = 128
 CHUNKS = S // CHUNK
@@ -55,7 +56,8 @@ def tile_picked_recall_gelu_p_kernel(tc, xT, s_words, s_scales, w1, w2, b, offs,
         x_codes = [keep.tile([P, CHUNK], U32, name=f"x_codes{i}", align_bytes=64) for i in range(CHUNKS)]
         x_scales = [keep.tile([P, CHUNK], U8, name=f"x_scales{i}", align_bytes=64) for i in range(CHUNKS)]
         picked_words = keep.tile([P, S], U32, name="picked_words", align_bytes=64)
-        picked_scales = keep.tile([P, S], U8, name="picked_scales", align_bytes=64)
+        picked_rows = keep.tile([P, S], U8, name="picked_rows", align_bytes=DMA_ALIGN)
+        picked_scales = keep.tile([P, S], U8, name="picked_scales", align_bytes=DMA_ALIGN)
         result = [keep.tile([P, M_TILES, CHUNK], F32, name=f"result{i}", align_bytes=DMA_ALIGN) for i in range(CHUNKS)]
         acc = [[psum.tile([P, CHUNK], F32, name=f"acc{i}_{m}") for m in range(M_TILES)] for i in range(CHUNKS)]
 
@@ -70,6 +72,10 @@ def tile_picked_recall_gelu_p_kernel(tc, xT, s_words, s_scales, w1, w2, b, offs,
                 nc.scalar.copy(out=dst_view, in_=src_view)
             else:
                 nc.vector.tensor_copy(out=dst_view, in_=src_view)
+
+        def load_x(n):
+            first, width = X_LOADS[n]
+            nc.sync.dma_start(out=x_loads[n][:], in_=x_rows[:, :, first:first + width])
 
         def round_x(i):
             if X_SCALAR_COLS[i] > 0:
@@ -93,19 +99,21 @@ def tile_picked_recall_gelu_p_kernel(tc, xT, s_words, s_scales, w1, w2, b, offs,
         nc.scalar.dma_start(out=bias_rows[0:P:QUADRANT, 0:QUADRANT * M_TILES].rearrange("q (m i) -> q m i", i=QUADRANT),
                             in_=b.rearrange("(m q i) o -> q m (i o)", q=P // QUADRANT, i=QUADRANT))
         nc.sync.dma_start(offsets[:], offs)
-        scale_rows = s_scales[0].bitcast(I32).rearrange("(q r) c -> r q c", r=4)
-        for r in range(4):
-            nc.sync.dma_start(out=store_scales[r:P:QUADRANT, :], in_=scale_rows[r])
+        nc.sync.dma_start(out=store_scales[0:P:SPREAD, :], in_=s_scales[0].bitcast(I32))
         nc.sync.dma_start(out=store_words[:], in_=s_words[0].rearrange("p c r -> p (c r)").bitcast(I32))
         nc.sync.dma_start(out=w1_raw[:], in_=w1.rearrange("(p j) n -> p j n", j=PACK))
-        for n, (first, width) in enumerate(X_LOADS):
-            nc.sync.dma_start(out=x_loads[n][:], in_=x_rows[:, :, first:first + width])
+        load_x(0)
 
         nc.scalar.activation(out=warm_out[:], in_=bias_rows[:, P - 1:P], func=GELU)
         nc.vector.transpose(bias[:], bias_rows[:])
 
         interleave(nc.scalar, w2_bf, w2_raw, 0, N)
-        nc.vector.tensor_copy(picked_scales[:], store_scales[:].bitcast(U8).indirect(offsets[:]))
+        nc.vector.tensor_copy(picked_rows[:], store_scales[:].bitcast(U8).indirect(offsets[:]))
+        nc.vector.tensor_copy(out=picked_scales[:].bitcast(I32), in_=picked_rows[:].bitcast(I32))
+        for r in range(1, 4):
+            nc.sync.dma_start(out=picked_scales[r:P:QUADRANT, :].bitcast(I32), in_=picked_rows[SPREAD * r:P:QUADRANT, :].bitcast(I32))
+        for n in range(1, len(X_LOADS)):
+            load_x(n)
         w2_codes = keep.tile([P, N], U32, name="w_codes1", tag="scale_bytes", align_bytes=DMA_ALIGN)
         quantize(w2_codes[:], w2_scales[:], w2_bf[:])
         for g0 in range(0, S, GATHER):

@@ -41,21 +41,21 @@ def tile_picked_recall_gelu_p_kernel(tc, xT, s_words, s_scales, w1, w2, b, offs,
         store_words = keep.tile([P, T], I32, name="store_words", align_bytes=DMA_ALIGN)
         store_scales = keep.tile([P, T // 4], I32, name="store_scales", tag="scale_bytes", align_bytes=DMA_ALIGN)
         bias_rows = keep.tile([P, P], F32, name="bias_rows", align_bytes=DMA_ALIGN)
-        bias = keep.tile([P, P], F32, name="bias", align_bytes=64)
+        bias = keep.tile([P, P], F32, name="bias", align_bytes=DMA_ALIGN)
         warm_out = keep.tile([P, 1], F32, name="warm_out")
         w1_raw = keep.tile([P, PACK, N], F32, name="w_raw0", align_bytes=DMA_ALIGN)
         w2_raw = keep.tile([P, PACK, N], F32, name="w_raw1", align_bytes=DMA_ALIGN)
-        w1_bf = keep.tile([P, N, PACK], BF16, name="w_bf0", align_bytes=64)
-        w2_bf = keep.tile([P, N, PACK], BF16, name="w_bf1", align_bytes=64)
-        w1_codes = keep.tile([P, N], U32, name="w_codes0", align_bytes=64)
-        w1_scales = keep.tile([P, N], U8, name="w_scales0", align_bytes=64)
-        w2_scales = keep.tile([P, N], U8, name="w_scales1", align_bytes=64)
+        w1_bf = keep.tile([P, N, PACK], BF16, name="w_bf0", align_bytes=DMA_ALIGN)
+        w2_bf = keep.tile([P, N, PACK], BF16, name="w_bf1", align_bytes=DMA_ALIGN)
+        w1_codes = keep.tile([P, N], U32, name="w_codes0", align_bytes=DMA_ALIGN)
+        w1_scales = keep.tile([P, N], U8, name="w_scales0", align_bytes=DMA_ALIGN)
+        w2_scales = keep.tile([P, N], U8, name="w_scales1", align_bytes=DMA_ALIGN)
         x_loads = [keep.tile([P, PACK, width], F32, name=f"x_load{n}", align_bytes=DMA_ALIGN)
                    for n, (first, width) in enumerate(X_LOADS)]
-        x_bf = [keep.tile([P, CHUNK, PACK], BF16, name=f"x_bf{i}", align_bytes=64) for i in range(CHUNKS)]
-        x_codes = [keep.tile([P, CHUNK], U32, name=f"x_codes{i}", align_bytes=64) for i in range(CHUNKS)]
-        x_scales = [keep.tile([P, CHUNK], U8, name=f"x_scales{i}", align_bytes=64) for i in range(CHUNKS)]
-        picked_words = keep.tile([P, S], U32, name="picked_words", align_bytes=64)
+        x_bf = [keep.tile([P, CHUNK, PACK], BF16, name=f"x_bf{i}", align_bytes=DMA_ALIGN) for i in range(CHUNKS)]
+        x_codes = [keep.tile([P, CHUNK], U32, name=f"x_codes{i}", align_bytes=DMA_ALIGN) for i in range(CHUNKS)]
+        x_scales = [keep.tile([P, CHUNK], U8, name=f"x_scales{i}", align_bytes=DMA_ALIGN) for i in range(CHUNKS)]
+        picked_words = keep.tile([P, S], U32, name="picked_words", align_bytes=DMA_ALIGN)
         picked_rows = keep.tile([P, S], U8, name="picked_rows", align_bytes=DMA_ALIGN)
         picked_scales = keep.tile([P, S], U8, name="picked_scales", align_bytes=DMA_ALIGN)
         result = [keep.tile([P, M_TILES, CHUNK], F32, name=f"result{i}", align_bytes=DMA_ALIGN) for i in range(CHUNKS)]

@@ -23,11 +23,11 @@ M_TILES = N // P
 CHUNK = 128
 CHUNKS = S // CHUNK
 LAST = CHUNKS - 1
-GATHER = 512
 LIST_ROWS = 16
 X_LOADS = ((0, 2 * CHUNK), (2 * CHUNK, CHUNK), (3 * CHUNK, CHUNK))
 W1_SCALAR_COLS = 176
 X_SCALAR_COLS = (48, 48, CHUNK, 0)
+WARM_COLS = (128, 64)
 LAST_PARTS = ((0, CHUNK // 2), (CHUNK // 2, CHUNK))
 
 
@@ -38,7 +38,7 @@ def tile_picked_recall_gelu_p_kernel(tc, xT, s_words, s_scales, w1, w2, b, offs,
         psum = ctx.enter_context(tc.psum_pool(name="psum", bufs=1))
 
         offsets = keep.tile([P, S // LIST_ROWS], U16, name="offsets", align_bytes=DMA_ALIGN)
-        store_words = keep.tile([P, T], I32, name="store_words", align_bytes=DMA_ALIGN)
+        store_words = keep.tile([P, T], I32, name="store_words", tag="words", align_bytes=DMA_ALIGN)
         store_scales = keep.tile([P, T // 4], I32, name="store_scales", tag="scale_bytes", align_bytes=DMA_ALIGN)
         bias_rows = keep.tile([P, P], F32, name="bias_rows", align_bytes=DMA_ALIGN)
         bias = keep.tile([P, P], F32, name="bias", align_bytes=DMA_ALIGN)
@@ -89,7 +89,7 @@ def tile_picked_recall_gelu_p_kernel(tc, xT, s_words, s_scales, w1, w2, b, offs,
 
         def product(i, m, w_codes, w_scales, codes, scales, first):
             rows = slice(m * P, (m + 1) * P)
-            nc.tensor.matmul_mx(out=acc[i][m][:], lhsT=w_codes[:, rows].bitcast(FP8X4), lhsT_scale=w_scales[:, rows],
+            nc.tensor.matmul_mx(out=acc[i][m][:], lhsT=w_codes[m].bitcast(FP8X4), lhsT_scale=w_scales[:, rows],
                                 rhs=codes.bitcast(FP8X4), rhs_scale=scales, start=first, stop=not first)
 
         nc.vector.memset(bias_rows[:], 0.0)
@@ -114,15 +114,12 @@ def tile_picked_recall_gelu_p_kernel(tc, xT, s_words, s_scales, w1, w2, b, offs,
             nc.sync.dma_start(out=picked_scales[r:P:QUADRANT, :].bitcast(I32), in_=picked_rows[SPREAD * r:P:QUADRANT, :].bitcast(I32))
         for n in range(1, len(X_LOADS)):
             load_x(n)
-        w2_codes = keep.tile([P, N], U32, name="w_codes1", tag="scale_bytes", align_bytes=DMA_ALIGN)
-        quantize(w2_codes[:], w2_scales[:], w2_bf[:])
-        for g0 in range(0, S, GATHER):
-            entries = offsets[:, g0 // LIST_ROWS:(g0 + GATHER) // LIST_ROWS]
-            nc.vector.tensor_copy(picked_words[:, g0:g0 + GATHER], store_words[:].bitcast(U32).indirect(entries))
-            for i in range(g0 // CHUNK, (g0 + GATHER) // CHUNK):
-                cols = slice(i * CHUNK, (i + 1) * CHUNK)
-                for m in range(M_TILES):
-                    product(i, m, w2_codes, w2_scales, picked_words[:, cols], picked_scales[:, cols], first=True)
+        w2_first = keep.tile([P, P], U32, name="w2_codes0", tag="scale_bytes", align_bytes=DMA_ALIGN)
+        quantize(w2_first[:], w2_scales[:, 0:P], w2_bf[:, 0:P, :])
+        nc.vector.tensor_copy(picked_words[:], store_words[:].bitcast(U32).indirect(offsets[:]))
+        w2_second = keep.tile([P, P], U32, name="w2_codes1", tag="words", align_bytes=DMA_ALIGN)
+        quantize(w2_second[:], w2_scales[:, P:N], w2_bf[:, P:N, :])
+        w2_codes = (w2_first[:], w2_second[:])
 
         interleave(nc.scalar, w1_bf, w1_raw, 0, P)
         interleave(nc.scalar, w1_bf, w1_raw, P, W1_SCALAR_COLS)
@@ -130,6 +127,13 @@ def tile_picked_recall_gelu_p_kernel(tc, xT, s_words, s_scales, w1, w2, b, offs,
         for m in range(M_TILES):
             rows = slice(m * P, (m + 1) * P)
             quantize(w1_codes[:, rows], w1_scales[:, rows], w1_bf[:, rows, :])
+        for m, width in enumerate(WARM_COLS):
+            nc.tensor.matmul_mx(out=acc[LAST][m][:, 0:width], lhsT=w2_first[:].bitcast(FP8X4), lhsT_scale=w2_scales[:, 0:P],
+                                rhs=w2_second[:, 0:width].bitcast(FP8X4), rhs_scale=w2_scales[:, P:P + width], start=True, stop=True)
+        for i in range(CHUNKS):
+            cols = slice(i * CHUNK, (i + 1) * CHUNK)
+            for m in range(M_TILES):
+                product(i, m, w2_codes, w2_scales, picked_words[:, cols], picked_scales[:, cols], first=True)
         round_x(0)
         round_x(1)
         for i in range(CHUNKS):
@@ -138,7 +142,7 @@ def tile_picked_recall_gelu_p_kernel(tc, xT, s_words, s_scales, w1, w2, b, offs,
             for lo, hi in LAST_PARTS if i == LAST else ((0, CHUNK),):
                 quantize(x_codes[i][:, lo:hi], x_scales[i][:, lo:hi], x_bf[i][:, lo:hi, :])
             for m in range(M_TILES):
-                product(i, m, w1_codes, w1_scales, x_codes[i][:], x_scales[i][:], first=False)
+                product(i, m, (w1_codes[:, 0:P], w1_codes[:, P:N]), w1_scales, x_codes[i][:], x_scales[i][:], first=False)
             for m in range(M_TILES):
                 nc.scalar.activation(out=result[i][:, m, :], in_=acc[i][m][:], func=GELU,
                                      bias=bias[:, QUADRANT * m:QUADRANT * m + 1])

@@ -102,7 +102,8 @@ def tile_picked_recall_gelu_p_kernel(tc, xT, s_words, s_scales, w1, w2, b, offs,
         nc.sync.dma_start(out=store_scales[0:P:SPREAD, :], in_=s_scales[0].bitcast(I32))
         nc.sync.dma_start(out=store_words[:], in_=s_words[0].rearrange("p c r -> p (c r)").bitcast(I32))
         nc.sync.dma_start(out=w1_raw[:], in_=w1.rearrange("(p j) n -> p j n", j=PACK))
-        load_x(0)
+        for n in range(len(X_LOADS)):
+            load_x(n)
 
         nc.scalar.activation(out=warm_out[:], in_=bias_rows[:, P - 1:P], func=GELU)
         nc.vector.transpose(bias[:], bias_rows[:])
@@ -111,9 +112,7 @@ def tile_picked_recall_gelu_p_kernel(tc, xT, s_words, s_scales, w1, w2, b, offs,
         nc.vector.tensor_copy(picked_rows[:], store_scales[:].bitcast(U8).indirect(offsets[:]))
         nc.vector.tensor_copy(out=picked_scales[:].bitcast(I32), in_=picked_rows[:].bitcast(I32))
         for r in range(1, 4):
-            nc.sync.dma_start(out=picked_scales[r:P:QUADRANT, :].bitcast(I32), in_=picked_rows[SPREAD * r:P:QUADRANT, :].bitcast(I32))
-        for n in range(1, len(X_LOADS)):
-            load_x(n)
+            nc.scalar.dma_start(out=picked_scales[r:P:QUADRANT, :].bitcast(I32), in_=picked_rows[SPREAD * r:P:QUADRANT, :].bitcast(I32))
         w2_first = keep.tile([P, P], U32, name="w2_codes0", tag="scale_bytes", align_bytes=DMA_ALIGN)
         quantize(w2_first[:], w2_scales[:, 0:P], w2_bf[:, 0:P, :])
         nc.vector.tensor_copy(picked_words[:], store_words[:].bitcast(U32).indirect(offsets[:]))

@@ -18,17 +18,19 @@ P = 128
 PACK = 4
 QUADRANT = 32
 DMA_ALIGN = 256
-SPREAD = 8
+ROWS = 16
 M_TILES = N // P
+LIST_ROWS = 16
 CHUNK = 128
 CHUNKS = S // CHUNK
 LAST = CHUNKS - 1
-LIST_ROWS = 16
+HALF = CHUNK // 2
 X_LOADS = ((0, 2 * CHUNK), (2 * CHUNK, CHUNK), (3 * CHUNK, CHUNK))
-W1_SCALAR_COLS = 176
-X_SCALAR_COLS = (48, 48, CHUNK, 0)
-WARM_COLS = (128, 64)
-LAST_PARTS = ((0, CHUNK // 2), (CHUNK // 2, CHUNK))
+GATHERS = 2
+W2_SCALAR_COLS = (64, 64)
+W1_SCALAR_COLS = (48, 48)
+FIRST_SCALAR_COLS = 96
+SECOND_SCALAR_COLS = 128
 
 
 def tile_picked_recall_gelu_p_kernel(tc, xT, s_words, s_scales, w1, w2, b, offs, out):
@@ -38,112 +40,114 @@ def tile_picked_recall_gelu_p_kernel(tc, xT, s_words, s_scales, w1, w2, b, offs,
         psum = ctx.enter_context(tc.psum_pool(name="psum", bufs=1))
 
         offsets = keep.tile([P, S // LIST_ROWS], U16, name="offsets", align_bytes=DMA_ALIGN)
-        store_words = keep.tile([P, T], I32, name="store_words", tag="words", align_bytes=DMA_ALIGN)
-        store_scales = keep.tile([P, T // 4], I32, name="store_scales", tag="scale_bytes", align_bytes=DMA_ALIGN)
+        store_words = keep.tile([P, T], I32, name="store_words", align_bytes=DMA_ALIGN)
+        store_scales = keep.tile([P, T // 4], I32, name="store_scales", align_bytes=DMA_ALIGN)
         bias_rows = keep.tile([P, P], F32, name="bias_rows", align_bytes=DMA_ALIGN)
         bias = keep.tile([P, P], F32, name="bias", align_bytes=DMA_ALIGN)
         warm_out = keep.tile([P, 1], F32, name="warm_out")
-        w1_raw = keep.tile([P, PACK, N], F32, name="w_raw0", align_bytes=DMA_ALIGN)
-        w2_raw = keep.tile([P, PACK, N], F32, name="w_raw1", align_bytes=DMA_ALIGN)
-        w1_bf = keep.tile([P, N, PACK], BF16, name="w_bf0", align_bytes=DMA_ALIGN)
-        w2_bf = keep.tile([P, N, PACK], BF16, name="w_bf1", align_bytes=DMA_ALIGN)
-        w1_codes = keep.tile([P, N], U32, name="w_codes0", align_bytes=DMA_ALIGN)
-        w1_scales = keep.tile([P, N], U8, name="w_scales0", align_bytes=DMA_ALIGN)
-        w2_scales = keep.tile([P, N], U8, name="w_scales1", align_bytes=DMA_ALIGN)
-        x_loads = [keep.tile([P, PACK, width], F32, name=f"x_load{n}", align_bytes=DMA_ALIGN)
-                   for n, (first, width) in enumerate(X_LOADS)]
-        x_bf = [keep.tile([P, CHUNK, PACK], BF16, name=f"x_bf{i}", align_bytes=DMA_ALIGN) for i in range(CHUNKS)]
-        x_codes = [keep.tile([P, CHUNK], U32, name=f"x_codes{i}", align_bytes=DMA_ALIGN) for i in range(CHUNKS)]
-        x_scales = [keep.tile([P, CHUNK], U8, name=f"x_scales{i}", align_bytes=DMA_ALIGN) for i in range(CHUNKS)]
+        w1_raw = keep.tile([P, PACK, N], F32, name="w1_raw", align_bytes=DMA_ALIGN)
+        w2_raw = keep.tile([P, PACK, N], F32, name="w2_raw", align_bytes=DMA_ALIGN)
+        w1_bf = keep.tile([P, N, PACK], BF16, name="w1_bf", align_bytes=DMA_ALIGN)
+        w2_bf = keep.tile([P, N, PACK], BF16, name="w2_bf", align_bytes=DMA_ALIGN)
+        w1_codes = keep.tile([P, N], U32, name="w1_codes", align_bytes=DMA_ALIGN)
+        w2_codes = keep.tile([P, N], U32, name="w2_codes", align_bytes=DMA_ALIGN)
+        w1_scales = keep.tile([P, N], U8, name="w1_scales", align_bytes=DMA_ALIGN)
+        w2_scales = keep.tile([P, N], U8, name="w2_scales", align_bytes=DMA_ALIGN)
+        x_raw = [keep.tile([P, PACK, width], F32, name=f"x_raw{n}", tag=f"x_raw{n}", align_bytes=DMA_ALIGN)
+                 for n, (first, width) in enumerate(X_LOADS)]
+        x_bf = keep.tile([P, S, PACK], BF16, name="x_bf", align_bytes=DMA_ALIGN)
+        x_codes = keep.tile([P, S], U32, name="x_codes", align_bytes=DMA_ALIGN)
+        x_scales = keep.tile([P, S], U8, name="x_scales", align_bytes=DMA_ALIGN)
         picked_words = keep.tile([P, S], U32, name="picked_words", align_bytes=DMA_ALIGN)
         picked_rows = keep.tile([P, S], U8, name="picked_rows", align_bytes=DMA_ALIGN)
         picked_scales = keep.tile([P, S], U8, name="picked_scales", align_bytes=DMA_ALIGN)
         result = [keep.tile([P, M_TILES, CHUNK], F32, name=f"result{i}", align_bytes=DMA_ALIGN) for i in range(CHUNKS)]
         acc = [[psum.tile([P, CHUNK], F32, name=f"acc{i}_{m}") for m in range(M_TILES)] for i in range(CHUNKS)]
 
-        x_raw = [x_loads[n][:, :, c:c + CHUNK] for n, (first, width) in enumerate(X_LOADS) for c in range(0, width, CHUNK)]
         x_rows = xT.rearrange("(p j) s -> p j s", j=PACK)
         out_rows = out.rearrange("(m p) s -> p m s", p=P)
+        tiles = [slice(m * P, (m + 1) * P) for m in range(M_TILES)]
+        chunks = [slice(i * CHUNK, (i + 1) * CHUNK) for i in range(CHUNKS)]
 
-        def interleave(eng, dst, src, lo, hi):
-            dst_view = dst[:, lo:hi, :].rearrange("p (c i) j -> p c j i", i=4)
-            src_view = src[:, :, lo:hi].rearrange("p j (c i) -> p c j i", i=4)
+        def interleave(eng, dst, src):
+            dst_view = dst.rearrange("p (c i) j -> p c j i", i=4)
+            src_view = src.rearrange("p j (c i) -> p c j i", i=4)
             if eng is nc.scalar:
                 nc.scalar.copy(out=dst_view, in_=src_view)
             else:
                 nc.vector.tensor_copy(out=dst_view, in_=src_view)
 
-        def load_x(n):
-            first, width = X_LOADS[n]
-            nc.sync.dma_start(out=x_loads[n][:], in_=x_rows[:, :, first:first + width])
+        def round_x(eng, n, lo, hi):
+            first = X_LOADS[n][0]
+            interleave(eng, x_bf[:, first + lo:first + hi, :], x_raw[n][:, :, lo:hi])
 
-        def round_x(i):
-            if X_SCALAR_COLS[i] > 0:
-                interleave(nc.scalar, x_bf[i], x_raw[i], 0, X_SCALAR_COLS[i])
-            if X_SCALAR_COLS[i] < CHUNK:
-                for lo, hi in LAST_PARTS if i == LAST else ((X_SCALAR_COLS[i], CHUNK),):
-                    interleave(nc.vector, x_bf[i], x_raw[i], lo, hi)
+        def round_w(w_bf, w_raw, scalar_cols):
+            for m in range(M_TILES):
+                cut = m * P + scalar_cols[m]
+                interleave(nc.scalar, w_bf[:, m * P:cut, :], w_raw[:, :, m * P:cut])
+                interleave(nc.vector, w_bf[:, cut:(m + 1) * P, :], w_raw[:, :, cut:(m + 1) * P])
 
-        def quantize(codes, scales, src):
-            nc.vector.quantize_mx(out=codes.bitcast(FP8X4), scales=scales, in_=src.rearrange("p c j -> p (c j)"))
+        def quantize(codes, scales, src, cols):
+            nc.vector.quantize_mx(out=codes[:, cols].bitcast(FP8X4), scales=scales[:, cols],
+                                  in_=src[:, cols, :].rearrange("p c j -> p (c j)"))
 
         def product(i, m, w_codes, w_scales, codes, scales, first):
-            rows = slice(m * P, (m + 1) * P)
-            nc.tensor.matmul_mx(out=acc[i][m][:], lhsT=w_codes[m].bitcast(FP8X4), lhsT_scale=w_scales[:, rows],
-                                rhs=codes.bitcast(FP8X4), rhs_scale=scales, start=first, stop=not first)
+            nc.tensor.matmul_mx(out=acc[i][m][:], lhsT=w_codes[:, tiles[m]].bitcast(FP8X4), lhsT_scale=w_scales[:, tiles[m]],
+                                rhs=codes[:, chunks[i]].bitcast(FP8X4), rhs_scale=scales[:, chunks[i]], start=first, stop=not first)
 
-        nc.vector.memset(bias_rows[:], 0.0)
-        nc.vector.memset(store_scales[:], 0)
-
-        nc.sync.dma_start(out=w2_raw[:], in_=w2.rearrange("(p j) n -> p j n", j=PACK))
-        nc.scalar.dma_start(out=bias_rows[0:P:QUADRANT, 0:QUADRANT * M_TILES].rearrange("q (m i) -> q m i", i=QUADRANT),
-                            in_=b.rearrange("(m q i) o -> q m (i o)", q=P // QUADRANT, i=QUADRANT))
-        nc.sync.dma_start(offsets[:], offs)
-        nc.sync.dma_start(out=store_scales[0:P:SPREAD, :], in_=s_scales[0].bitcast(I32))
-        nc.sync.dma_start(out=store_words[:], in_=s_words[0].rearrange("p c r -> p (c r)").bitcast(I32))
-        nc.sync.dma_start(out=w1_raw[:], in_=w1.rearrange("(p j) n -> p j n", j=PACK))
-        for n in range(len(X_LOADS)):
-            load_x(n)
-
-        nc.scalar.activation(out=warm_out[:], in_=bias_rows[:, P - 1:P], func=GELU)
-        nc.vector.transpose(bias[:], bias_rows[:])
-
-        interleave(nc.scalar, w2_bf, w2_raw, 0, N)
-        nc.vector.tensor_copy(picked_rows[:], store_scales[:].bitcast(U8).indirect(offsets[:]))
-        nc.vector.tensor_copy(out=picked_scales[:].bitcast(I32), in_=picked_rows[:].bitcast(I32))
-        for r in range(1, 4):
-            nc.scalar.dma_start(out=picked_scales[r:P:QUADRANT, :].bitcast(I32), in_=picked_rows[SPREAD * r:P:QUADRANT, :].bitcast(I32))
-        w2_first = keep.tile([P, P], U32, name="w2_codes0", tag="scale_bytes", align_bytes=DMA_ALIGN)
-        quantize(w2_first[:], w2_scales[:, 0:P], w2_bf[:, 0:P, :])
-        nc.vector.tensor_copy(picked_words[:], store_words[:].bitcast(U32).indirect(offsets[:]))
-        w2_second = keep.tile([P, P], U32, name="w2_codes1", tag="words", align_bytes=DMA_ALIGN)
-        quantize(w2_second[:], w2_scales[:, P:N], w2_bf[:, P:N, :])
-        w2_codes = (w2_first[:], w2_second[:])
-
-        interleave(nc.scalar, w1_bf, w1_raw, 0, P)
-        interleave(nc.scalar, w1_bf, w1_raw, P, W1_SCALAR_COLS)
-        interleave(nc.vector, w1_bf, w1_raw, W1_SCALAR_COLS, N)
-        for m in range(M_TILES):
-            rows = slice(m * P, (m + 1) * P)
-            quantize(w1_codes[:, rows], w1_scales[:, rows], w1_bf[:, rows, :])
-        for m, width in enumerate(WARM_COLS):
-            nc.tensor.matmul_mx(out=acc[LAST][m][:, 0:width], lhsT=w2_first[:].bitcast(FP8X4), lhsT_scale=w2_scales[:, 0:P],
-                                rhs=w2_second[:, 0:width].bitcast(FP8X4), rhs_scale=w2_scales[:, P:P + width], start=True, stop=True)
-        for i in range(CHUNKS):
-            cols = slice(i * CHUNK, (i + 1) * CHUNK)
+        def close_chunk(i):
             for m in range(M_TILES):
-                product(i, m, w2_codes, w2_scales, picked_words[:, cols], picked_scales[:, cols], first=True)
-        round_x(0)
-        round_x(1)
-        for i in range(CHUNKS):
-            if 1 <= i < LAST:
-                round_x(i + 1)
-            for lo, hi in LAST_PARTS if i == LAST else ((0, CHUNK),):
-                quantize(x_codes[i][:, lo:hi], x_scales[i][:, lo:hi], x_bf[i][:, lo:hi, :])
-            for m in range(M_TILES):
-                product(i, m, (w1_codes[:, 0:P], w1_codes[:, P:N]), w1_scales, x_codes[i][:], x_scales[i][:], first=False)
+                product(i, m, w1_codes, w1_scales, x_codes, x_scales, first=False)
             for m in range(M_TILES):
                 nc.scalar.activation(out=result[i][:, m, :], in_=acc[i][m][:], func=GELU,
                                      bias=bias[:, QUADRANT * m:QUADRANT * m + 1])
-            cols = slice(i * CHUNK, (i + 1) * CHUNK)
-            nc.sync.dma_start(out=out_rows[:, :, cols], in_=result[i][:])
+            (nc.scalar if i == LAST else nc.sync).dma_start(out=out_rows[:, :, chunks[i]], in_=result[i][:])
+
+        nc.vector.memset(bias_rows[:], 0.0)
+        nc.vector.memset(store_scales[0:ROWS, :], 0)
+        nc.gpsimd.memset(store_scales[QUADRANT:2 * QUADRANT, :], 0)
+        nc.vector.memset(store_scales[2 * QUADRANT:P, :], 0)
+        nc.vector.memset(picked_scales[:].bitcast(I32), 0)
+
+        nc.sync.dma_start(offsets[:], offs)
+        nc.scalar.dma_start(out=store_scales[ROWS:2 * ROWS, :], in_=s_scales[0].bitcast(I32))
+        nc.sync.dma_start(out=store_words[:], in_=s_words[0].rearrange("p c r -> p (c r)").bitcast(I32))
+        nc.sync.dma_start(out=bias_rows[0:P:QUADRANT, 0:QUADRANT * M_TILES].rearrange("q (m i) -> q m i", i=QUADRANT),
+                          in_=b.rearrange("(m q i) o -> q m (i o)", q=P // QUADRANT, i=QUADRANT))
+        nc.sync.dma_start(out=w2_raw[:], in_=w2.rearrange("(p j) n -> p j n", j=PACK))
+        nc.sync.dma_start(out=w1_raw[:], in_=w1.rearrange("(p j) n -> p j n", j=PACK))
+
+        nc.scalar.activation(out=warm_out[:], in_=bias_rows[:, P - 1:P], func=GELU)
+
+        nc.vector.tensor_copy(picked_rows[:], store_scales[:].bitcast(U8).indirect(offsets[:]))
+        for r in range(4):
+            nc.sync.dma_start(out=picked_scales[r:P:QUADRANT, :].bitcast(I32), in_=picked_rows[ROWS + r:2 * ROWS:4, :].bitcast(I32))
+        for n, (first, width) in enumerate(X_LOADS):
+            nc.sync.dma_start(out=x_raw[n][:], in_=x_rows[:, :, first:first + width])
+        nc.vector.transpose(bias[:], bias_rows[:])
+        for lo in range(0, S, S // GATHERS):
+            nc.vector.tensor_copy(picked_words[:, lo:lo + S // GATHERS],
+                                  store_words[:].bitcast(U32).indirect(offsets[:, lo // LIST_ROWS:(lo + S // GATHERS) // LIST_ROWS]))
+        round_w(w2_bf, w2_raw, W2_SCALAR_COLS)
+        for m in range(M_TILES):
+            quantize(w2_codes, w2_scales, w2_bf, tiles[m])
+        for i in range(CHUNKS):
+            for m in range(M_TILES):
+                product(i, m, w2_codes, w2_scales, picked_words, picked_scales, first=True)
+        round_w(w1_bf, w1_raw, W1_SCALAR_COLS)
+        for m in range(M_TILES):
+            quantize(w1_codes, w1_scales, w1_bf, tiles[m])
+
+        round_x(nc.scalar, 0, 0, FIRST_SCALAR_COLS)
+        round_x(nc.vector, 0, FIRST_SCALAR_COLS, 2 * CHUNK)
+        round_x(nc.scalar, 1, 0, SECOND_SCALAR_COLS)
+        for i in (1, 0):
+            quantize(x_codes, x_scales, x_bf, chunks[i])
+            close_chunk(i)
+        for lo in (0, HALF):
+            round_x(nc.vector, 2, lo, lo + HALF)
+        quantize(x_codes, x_scales, x_bf, chunks[2])
+        close_chunk(2)
+        for lo in (0, HALF):
+            quantize(x_codes, x_scales, x_bf, slice(LAST * CHUNK + lo, LAST * CHUNK + lo + HALF))
+        close_chunk(LAST)

@@ -61,7 +61,9 @@ def tile_picked_recall_gelu_p_kernel(tc, xT, s_words, s_scales, w1, w2, b, offs,
         picked_words = keep.tile([P, S], U32, name="picked_words", align_bytes=DMA_ALIGN)
         picked_rows = keep.tile([P, S], U8, name="picked_rows", align_bytes=DMA_ALIGN)
         picked_scales = keep.tile([P, S], U8, name="picked_scales", align_bytes=DMA_ALIGN)
-        result = [keep.tile([P, M_TILES, CHUNK], F32, name=f"result{i}", align_bytes=DMA_ALIGN) for i in range(CHUNKS)]
+        early = keep.tile([P, M_TILES, 2 * CHUNK], F32, name="early", align_bytes=DMA_ALIGN)
+        late = [keep.tile([P, M_TILES, CHUNK], F32, name=f"late{i}", align_bytes=DMA_ALIGN) for i in range(2)]
+        result = [early[:, :, chunks_of] for chunks_of in (slice(0, CHUNK), slice(CHUNK, 2 * CHUNK))] + [tile[:] for tile in late]
         acc = [[psum.tile([P, CHUNK], F32, name=f"acc{i}_{m}") for m in range(M_TILES)] for i in range(CHUNKS)]
 
         x_rows = xT.rearrange("(p j) s -> p j s", j=PACK)
@@ -101,7 +103,10 @@ def tile_picked_recall_gelu_p_kernel(tc, xT, s_words, s_scales, w1, w2, b, offs,
             for m in range(M_TILES):
                 nc.scalar.activation(out=result[i][:, m, :], in_=acc[i][m][:], func=GELU,
                                      bias=bias[:, QUADRANT * m:QUADRANT * m + 1])
-            (nc.scalar if i == LAST else nc.sync).dma_start(out=out_rows[:, :, chunks[i]], in_=result[i][:])
+            if i == 0:
+                nc.sync.dma_start(out=out_rows[:, :, 0:2 * CHUNK], in_=early[:])
+            if i > 1:
+                nc.sync.dma_start(out=out_rows[:, :, chunks[i]], in_=result[i])
 
         nc.vector.memset(bias_rows[:], 0.0)
         nc.vector.memset(store_scales[0:ROWS, :], 0)

@@ -109,13 +109,12 @@ def tile_picked_recall_gelu_p_kernel(tc, xT, s_words, s_scales, w1, w2, b, offs,
                 nc.sync.dma_start(out=out_rows[:, :, chunks[i]], in_=result[i])
 
         nc.vector.memset(bias_rows[:], 0.0)
-        nc.vector.memset(store_scales[0:ROWS, :], 0)
-        nc.gpsimd.memset(store_scales[QUADRANT:2 * QUADRANT, :], 0)
-        nc.vector.memset(store_scales[2 * QUADRANT:P, :], 0)
+        nc.vector.memset(store_scales[0:P - QUADRANT, :], 0)
+        nc.gpsimd.memset(store_scales[P - QUADRANT:P - ROWS, :], 0)
         nc.vector.memset(picked_scales[:].bitcast(I32), 0)
 
         nc.sync.dma_start(offsets[:], offs)
-        nc.scalar.dma_start(out=store_scales[ROWS:2 * ROWS, :], in_=s_scales[0].bitcast(I32))
+        nc.scalar.dma_start(out=store_scales[P - ROWS:P, :], in_=s_scales[0].bitcast(I32))
         nc.sync.dma_start(out=store_words[:], in_=s_words[0].rearrange("p c r -> p (c r)").bitcast(I32))
         nc.sync.dma_start(out=bias_rows[0:P:QUADRANT, 0:QUADRANT * M_TILES].rearrange("q (m i) -> q m i", i=QUADRANT),
                           in_=b.rearrange("(m q i) o -> q m (i o)", q=P // QUADRANT, i=QUADRANT))
@@ -126,7 +125,7 @@ def tile_picked_recall_gelu_p_kernel(tc, xT, s_words, s_scales, w1, w2, b, offs,
 
         nc.vector.tensor_copy(picked_rows[:], store_scales[:].bitcast(U8).indirect(offsets[:]))
         for r in range(4):
-            nc.sync.dma_start(out=picked_scales[r:P:QUADRANT, :].bitcast(I32), in_=picked_rows[ROWS + r:2 * ROWS:4, :].bitcast(I32))
+            nc.sync.dma_start(out=picked_scales[r:P:QUADRANT, :].bitcast(I32), in_=picked_rows[P - ROWS + r:P:4, :].bitcast(I32))
         for n, (first, width) in enumerate(X_LOADS):
             nc.sync.dma_start(out=x_raw[n][:], in_=x_rows[:, :, first:first + width])
         nc.vector.transpose(bias[:], bias_rows[:])

@@ -30,7 +30,6 @@ GATHERS = 2
 W2_SCALAR_COLS = (64, 64)
 W1_SCALAR_COLS = (48, 48)
 FIRST_SCALAR_COLS = 96
-SECOND_SCALAR_COLS = 128
 
 
 def tile_picked_recall_gelu_p_kernel(tc, xT, s_words, s_scales, w1, w2, b, offs, out):
@@ -144,13 +143,15 @@ def tile_picked_recall_gelu_p_kernel(tc, xT, s_words, s_scales, w1, w2, b, offs,
 
         round_x(nc.scalar, 0, 0, FIRST_SCALAR_COLS)
         round_x(nc.vector, 0, FIRST_SCALAR_COLS, 2 * CHUNK)
-        round_x(nc.scalar, 1, 0, SECOND_SCALAR_COLS)
+        for lo in (0, HALF):
+            round_x(nc.scalar, 1, lo, lo + HALF)
         for i in (1, 0):
             quantize(x_codes, x_scales, x_bf, chunks[i])
             close_chunk(i)
+        quantize(x_codes, x_scales, x_bf, slice(2 * CHUNK, 2 * CHUNK + HALF))
         for lo in (0, HALF):
             round_x(nc.vector, 2, lo, lo + HALF)
-        quantize(x_codes, x_scales, x_bf, chunks[2])
+        quantize(x_codes, x_scales, x_bf, slice(2 * CHUNK + HALF, 3 * CHUNK))
         close_chunk(2)
         for lo in (0, HALF):
             quantize(x_codes, x_scales, x_bf, slice(LAST * CHUNK + lo, LAST * CHUNK + lo + HALF))

@@ -30,6 +30,7 @@ GATHERS = 2
 W2_SCALAR_COLS = (64, 64)
 W1_SCALAR_COLS = (48, 48)
 FIRST_SCALAR_COLS = 96
+SECOND_SCALAR_COLS = 96
 
 
 def tile_picked_recall_gelu_p_kernel(tc, xT, s_words, s_scales, w1, w2, b, offs, out):
@@ -142,12 +143,14 @@ def tile_picked_recall_gelu_p_kernel(tc, xT, s_words, s_scales, w1, w2, b, offs,
             quantize(w1_codes, w1_scales, w1_bf, tiles[m])
 
         round_x(nc.scalar, 0, 0, FIRST_SCALAR_COLS)
-        round_x(nc.vector, 0, FIRST_SCALAR_COLS, 2 * CHUNK)
-        for lo in (0, HALF):
-            round_x(nc.scalar, 1, lo, lo + HALF)
+        round_x(nc.vector, 0, CHUNK, 2 * CHUNK)
+        round_x(nc.vector, 0, FIRST_SCALAR_COLS, CHUNK)
+        round_x(nc.scalar, 1, 0, HALF)
+        round_x(nc.scalar, 1, HALF, SECOND_SCALAR_COLS)
         for i in (1, 0):
             quantize(x_codes, x_scales, x_bf, chunks[i])
             close_chunk(i)
+        round_x(nc.vector, 1, SECOND_SCALAR_COLS, CHUNK)
         quantize(x_codes, x_scales, x_bf, slice(2 * CHUNK, 2 * CHUNK + HALF))
         for lo in (0, HALF):
             round_x(nc.vector, 2, lo, lo + HALF)

@@ -27,6 +27,7 @@ LAST = CHUNKS - 1
 HALF = CHUNK // 2
 X_LOADS = ((0, 2 * CHUNK), (2 * CHUNK, CHUNK), (3 * CHUNK, CHUNK))
 GATHERS = 2
+PIECE = 4096
 W2_SCALAR_COLS = (64, 64)
 W1_SCALAR_COLS = (48, 48)
 FIRST_SCALAR_COLS = 96
@@ -115,7 +116,8 @@ def tile_picked_recall_gelu_p_kernel(tc, xT, s_words, s_scales, w1, w2, b, offs,
 
         nc.sync.dma_start(offsets[:], offs)
         nc.scalar.dma_start(out=store_scales[P - ROWS:P, :], in_=s_scales[0].bitcast(I32))
-        nc.sync.dma_start(out=store_words[:], in_=s_words[0].rearrange("p c r -> p (c r)").bitcast(I32))
+        nc.sync.dma_start(out=store_words[:], in_=s_words[0].rearrange("p c r -> p (c r)").bitcast(I32),
+                          max_dma_last_dim=PIECE)
         nc.sync.dma_start(out=bias_rows[0:P:QUADRANT, 0:QUADRANT * M_TILES].rearrange("q (m i) -> q m i", i=QUADRANT),
                           in_=b.rearrange("(m q i) o -> q m (i o)", q=P // QUADRANT, i=QUADRANT))
         nc.sync.dma_start(out=w2_raw[:], in_=w2.rearrange("(p j) n -> p j n", j=PACK))

from contextlib import ExitStack

import concourse.mybir as mybir

K, T, S, N = 512, 2048, 512, 256
FLOPS = 2 * 2 * K * N * S

F32 = mybir.dt.float32
BF16 = mybir.dt.bfloat16
I32 = mybir.dt.int32
U32 = mybir.dt.uint32
U16 = mybir.dt.uint16
U8 = mybir.dt.uint8
FP8X4 = mybir.dt.float8_e4m3fn_x4
GELU = mybir.ActivationFunctionType.Gelu_apprx_tanh

P = 128
PACK = 4
QUADRANT = 32
DMA_ALIGN = 256
ROWS = 16
M_TILES = N // P
LIST_ROWS = 16
CHUNK = 128
CHUNKS = S // CHUNK
LAST = CHUNKS - 1
HALF = CHUNK // 2
X_LOADS = ((0, 2 * CHUNK), (2 * CHUNK, CHUNK), (3 * CHUNK, CHUNK))
GATHERS = 2
PIECE = 4096
W2_SCALAR_COLS = (64, 64)
W1_SCALAR_COLS = (48, 48)
FIRST_SCALAR_COLS = 96
SECOND_SCALAR_COLS = 96


def tile_picked_recall_gelu_p_kernel(tc, xT, s_words, s_scales, w1, w2, b, offs, out):
    nc = tc.nc
    with ExitStack() as ctx:
        keep = ctx.enter_context(tc.tile_pool(name="keep", bufs=1))
        psum = ctx.enter_context(tc.psum_pool(name="psum", bufs=1))

        offsets = keep.tile([P, S // LIST_ROWS], U16, name="offsets", align_bytes=DMA_ALIGN)
        store_words = keep.tile([P, T], I32, name="store_words", align_bytes=DMA_ALIGN)
        store_scales = keep.tile([P, T // 4], I32, name="store_scales", align_bytes=DMA_ALIGN)
        bias_rows = keep.tile([P, P], F32, name="bias_rows", align_bytes=DMA_ALIGN)
        bias = keep.tile([P, P], F32, name="bias", align_bytes=DMA_ALIGN)
        warm_out = keep.tile([P, 1], F32, name="warm_out")
        w1_raw = keep.tile([P, PACK, N], F32, name="w1_raw", align_bytes=DMA_ALIGN)
        w2_raw = keep.tile([P, PACK, N], F32, name="w2_raw", align_bytes=DMA_ALIGN)
        w1_bf = keep.tile([P, N, PACK], BF16, name="w1_bf", align_bytes=DMA_ALIGN)
        w2_bf = keep.tile([P, N, PACK], BF16, name="w2_bf", align_bytes=DMA_ALIGN)
        w1_codes = keep.tile([P, N], U32, name="w1_codes", align_bytes=DMA_ALIGN)
        w2_codes = keep.tile([P, N], U32, name="w2_codes", align_bytes=DMA_ALIGN)
        w1_scales = keep.tile([P, N], U8, name="w1_scales", align_bytes=DMA_ALIGN)
        w2_scales = keep.tile([P, N], U8, name="w2_scales", align_bytes=DMA_ALIGN)
        x_raw = [keep.tile([P, PACK, width], F32, name=f"x_raw{n}", tag=f"x_raw{n}", align_bytes=DMA_ALIGN)
                 for n, (first, width) in enumerate(X_LOADS)]
        x_bf = keep.tile([P, S, PACK], BF16, name="x_bf", align_bytes=DMA_ALIGN)
        x_codes = keep.tile([P, S], U32, name="x_codes", align_bytes=DMA_ALIGN)
        x_scales = keep.tile([P, S], U8, name="x_scales", align_bytes=DMA_ALIGN)
        picked_words = keep.tile([P, S], U32, name="picked_words", align_bytes=DMA_ALIGN)
        picked_rows = keep.tile([P, S], U8, name="picked_rows", align_bytes=DMA_ALIGN)
        picked_scales = keep.tile([P, S], U8, name="picked_scales", align_bytes=DMA_ALIGN)
        early = keep.tile([P, M_TILES, 2 * CHUNK], F32, name="early", align_bytes=DMA_ALIGN)
        late = [keep.tile([P, M_TILES, CHUNK], F32, name=f"late{i}", align_bytes=DMA_ALIGN) for i in range(2)]
        result = [early[:, :, chunks_of] for chunks_of in (slice(0, CHUNK), slice(CHUNK, 2 * CHUNK))] + [tile[:] for tile in late]
        acc = [[psum.tile([P, CHUNK], F32, name=f"acc{i}_{m}") for m in range(M_TILES)] for i in range(CHUNKS)]

        x_rows = xT.rearrange("(p j) s -> p j s", j=PACK)
        out_rows = out.rearrange("(m p) s -> p m s", p=P)
        tiles = [slice(m * P, (m + 1) * P) for m in range(M_TILES)]
        chunks = [slice(i * CHUNK, (i + 1) * CHUNK) for i in range(CHUNKS)]

        def interleave(eng, dst, src):
            dst_view = dst.rearrange("p (c i) j -> p c j i", i=4)
            src_view = src.rearrange("p j (c i) -> p c j i", i=4)
            if eng is nc.scalar:
                nc.scalar.copy(out=dst_view, in_=src_view)
            else:
                nc.vector.tensor_copy(out=dst_view, in_=src_view)

        def round_x(eng, n, lo, hi):
            first = X_LOADS[n][0]
            interleave(eng, x_bf[:, first + lo:first + hi, :], x_raw[n][:, :, lo:hi])

        def round_w(w_bf, w_raw, scalar_cols):
            for m in range(M_TILES):
                cut = m * P + scalar_cols[m]
                interleave(nc.scalar, w_bf[:, m * P:cut, :], w_raw[:, :, m * P:cut])
                interleave(nc.vector, w_bf[:, cut:(m + 1) * P, :], w_raw[:, :, cut:(m + 1) * P])

        def quantize(codes, scales, src, cols):
            nc.vector.quantize_mx(out=codes[:, cols].bitcast(FP8X4), scales=scales[:, cols],
                                  in_=src[:, cols, :].rearrange("p c j -> p (c j)"))

        def product(i, m, w_codes, w_scales, codes, scales, first):
            nc.tensor.matmul_mx(out=acc[i][m][:], lhsT=w_codes[:, tiles[m]].bitcast(FP8X4), lhsT_scale=w_scales[:, tiles[m]],
                                rhs=codes[:, chunks[i]].bitcast(FP8X4), rhs_scale=scales[:, chunks[i]], start=first, stop=not first)

        def close_chunk(i):
            for m in range(M_TILES):
                product(i, m, w1_codes, w1_scales, x_codes, x_scales, first=False)
            for m in range(M_TILES):
                nc.scalar.activation(out=result[i][:, m, :], in_=acc[i][m][:], func=GELU,
                                     bias=bias[:, QUADRANT * m:QUADRANT * m + 1])
            if i == 0:
                nc.sync.dma_start(out=out_rows[:, :, 0:2 * CHUNK], in_=early[:])
            if i > 1:
                nc.sync.dma_start(out=out_rows[:, :, chunks[i]], in_=result[i])

        nc.vector.memset(bias_rows[:], 0.0)
        nc.vector.memset(store_scales[0:P - QUADRANT, :], 0)
        nc.gpsimd.memset(store_scales[P - QUADRANT:P - ROWS, :], 0)
        nc.vector.memset(picked_scales[:].bitcast(I32), 0)

        nc.sync.dma_start(offsets[:], offs)
        nc.scalar.dma_start(out=store_scales[P - ROWS:P, :], in_=s_scales[0].bitcast(I32))
        nc.sync.dma_start(out=store_words[:], in_=s_words[0].rearrange("p c r -> p (c r)").bitcast(I32),
                          max_dma_last_dim=PIECE)
        nc.sync.dma_start(out=bias_rows[0:P:QUADRANT, 0:QUADRANT * M_TILES].rearrange("q (m i) -> q m i", i=QUADRANT),
                          in_=b.rearrange("(m q i) o -> q m (i o)", q=P // QUADRANT, i=QUADRANT))
        nc.sync.dma_start(out=w2_raw[:], in_=w2.rearrange("(p j) n -> p j n", j=PACK))
        nc.sync.dma_start(out=w1_raw[:], in_=w1.rearrange("(p j) n -> p j n", j=PACK))

        nc.scalar.activation(out=warm_out[:], in_=bias_rows[:, P - 1:P], func=GELU)

        nc.vector.tensor_copy(picked_rows[:], store_scales[:].bitcast(U8).indirect(offsets[:]))
        for r in range(4):
            nc.sync.dma_start(out=picked_scales[r:P:QUADRANT, :].bitcast(I32), in_=picked_rows[P - ROWS + r:P:4, :].bitcast(I32))
        for n, (first, width) in enumerate(X_LOADS):
            nc.sync.dma_start(out=x_raw[n][:], in_=x_rows[:, :, first:first + width])
        nc.vector.transpose(bias[:], bias_rows[:])
        for lo in range(0, S, S // GATHERS):
            nc.vector.tensor_copy(picked_words[:, lo:lo + S // GATHERS],
                                  store_words[:].bitcast(U32).indirect(offsets[:, lo // LIST_ROWS:(lo + S // GATHERS) // LIST_ROWS]))
        round_w(w2_bf, w2_raw, W2_SCALAR_COLS)
        for m in range(M_TILES):
            quantize(w2_codes, w2_scales, w2_bf, tiles[m])
        for i in range(CHUNKS):
            for m in range(M_TILES):
                product(i, m, w2_codes, w2_scales, picked_words, picked_scales, first=True)
        round_w(w1_bf, w1_raw, W1_SCALAR_COLS)
        for m in range(M_TILES):
            quantize(w1_codes, w1_scales, w1_bf, tiles[m])

        round_x(nc.scalar, 0, 0, FIRST_SCALAR_COLS)
        round_x(nc.vector, 0, CHUNK, 2 * CHUNK)
        round_x(nc.vector, 0, FIRST_SCALAR_COLS, CHUNK)
        round_x(nc.scalar, 1, 0, HALF)
        round_x(nc.scalar, 1, HALF, SECOND_SCALAR_COLS)
        for i in (1, 0):
            quantize(x_codes, x_scales, x_bf, chunks[i])
            close_chunk(i)
        round_x(nc.vector, 1, SECOND_SCALAR_COLS, CHUNK)
        quantize(x_codes, x_scales, x_bf, slice(2 * CHUNK, 2 * CHUNK + HALF))
        for lo in (0, HALF):
            round_x(nc.vector, 2, lo, lo + HALF)
        quantize(x_codes, x_scales, x_bf, slice(2 * CHUNK + HALF, 3 * CHUNK))
        close_chunk(2)
        for lo in (0, HALF):
            quantize(x_codes, x_scales, x_bf, slice(LAST * CHUNK + lo, LAST * CHUNK + lo + HALF))
        close_chunk(LAST)
